import numpy as np
import ml_dtypes


def mxq(x, axis, fmt="e4m3"):
    dtype, down = {"e4m3": (ml_dtypes.float8_e4m3fn, 7), "e5m2": (ml_dtypes.float8_e5m2, 14)}[fmt]
    v = np.moveaxis(np.asarray(x, np.float32).astype(ml_dtypes.bfloat16).astype(np.float64), axis, -1)
    blocks = v.reshape(v.shape[:-1] + (-1, 32))
    amax = np.abs(blocks).max(-1, keepdims=True)
    byte = np.maximum(np.where(amax > 0, np.frexp(amax)[1] - 1 + 127, 0) - down, 1)
    scale = np.exp2(byte - 127.0)
    codes = (blocks / scale).astype(np.float32).astype(dtype).astype(np.float64)
    return np.moveaxis((codes * scale).reshape(v.shape), -1, axis)


WIDE = False


def mx_kscale(k):
    if not WIDE:
        return np.ones(k)
    levels = np.array([10, -10, 5, -5, 0])
    if k % 512:
        return np.exp2(np.random.permutation(np.resize(levels, k // 32))).repeat(32)
    a = np.empty((k // 512, 16))
    for p in range(k // 512):
        a[p, :8] = np.random.permutation(np.resize(levels, 8))
        for g in range(8):
            far = levels[np.abs(levels - a[p, g]) >= 10]
            a[p, g + 8] = far[np.random.randint(len(far))]
    return np.exp2(a.ravel()).repeat(32)


def f64(x):
    return np.asarray(x).astype(np.float64)


def striped(idx):
    return np.tile(np.asarray(idx).reshape(-1, 16).T, (8, 1)).astype(np.uint16)


def unstriped(offs):
    return offs[:16].T.reshape(-1).astype(np.int64)


def striped8(idx):
    return np.asarray(idx).reshape(8, -1, 16).transpose(0, 2, 1).reshape(128, -1).astype(np.uint16)


def unstriped8(offs):
    return offs.reshape(8, 16, -1).transpose(0, 2, 1).reshape(8, -1).astype(np.int64)


def pick8(x, idx, run):
    r = np.arange(len(x))
    return x[r[:, None], idx[r % (8 * run) // run]]


E2M1 = np.array([0.0, 0.5, 1.0, 1.5, 2.0, 3.0, 4.0, 6.0, -0.0, -0.5, -1.0, -1.5, -2.0, -3.0, -4.0, -6.0])


def pack_weight(w, fmt):
    k, n = w.shape
    w = f64(np.asarray(w, np.float32).astype(ml_dtypes.bfloat16)).reshape(k // 32, 32, n)
    amax = np.abs(w).max(1)
    if fmt == "e4m3":
        byte = np.frexp(amax)[1] - 1 + 127 - 7
    else:
        mant, ex = np.frexp(amax / 6.0)
        byte = np.where(mant > 0.5, ex, ex - 1) + 127
    byte = np.clip(np.where(amax > 0, byte, 1), 1, 254)
    scaled = (w * np.exp2(127.0 - byte)[:, None, :]).reshape(k, n).astype(np.float32)
    by_word = np.ascontiguousarray(scaled.reshape(k // 512, 128, 4, n).transpose(0, 1, 3, 2))
    if fmt == "e4m3":
        words = by_word.astype(ml_dtypes.float8_e4m3fn).view(np.uint8)
    else:
        c = by_word.astype(ml_dtypes.float4_e2m1fn).view(np.uint8) & 0xF
        words = (c[..., 0::2] | (c[..., 1::2] << 4)).reshape(k // 512, 128, 2 * n)
    return np.ascontiguousarray(words), np.ascontiguousarray(byte.astype(np.uint8).reshape(k // 512, 16, n))


def unpack_weight(words, scales, fmt):
    g, _, n = scales.shape
    words = np.ascontiguousarray(words).reshape(g, 128, n, -1)
    if fmt == "e4m3":
        vals = words.view(ml_dtypes.float8_e4m3fn).astype(np.float64)
    else:
        nib = np.empty((g, 128, n, 4), np.uint8)
        nib[..., 0::2] = words & 0xF
        nib[..., 1::2] = words >> 4
        vals = E2M1[nib]
    vals = vals * np.repeat(np.exp2(scales.astype(np.float64) - 127.0), 8, axis=1)[..., None]
    return vals.transpose(0, 1, 3, 2).reshape(g * 512, n)


K, J, R, T, O, C, N, S, Z, U = 512, 512, 512, 2048, 256, 1024, 256, 512, 1024, 128


def setup_inputs():
    n = np.random.standard_normal
    idx = np.stack([np.random.permutation(T)[:J] for _ in range(8)])
    idx2 = np.stack([np.random.permutation(C)[:J] for _ in range(8)])
    idx3 = np.stack([np.random.permutation(C)[:O] for _ in range(8)])
    idx4 = np.stack([np.random.permutation(C)[:O] for _ in range(8)])
    idx5 = np.random.permutation(Z)[:O]
    idx6 = np.stack([np.random.permutation(O)[:U] for _ in range(8)])
    idx7 = np.random.permutation(O)[:U]
    fk = mx_kscale(K)
    fr = mx_kscale(R)
    fs = mx_kscale(S)
    wp = pack_weight(n((K, R)) * 1 / np.sqrt(K) / fk[:, None] * fr, "e4m3")
    wbp = pack_weight(n((R, N)) * 1 / np.sqrt(R) / fr[:, None], "e2m1")
    xrp = pack_weight(n((S, Z)) / fs[:, None], "e2m1")
    wsp = pack_weight(n((S, N)) * 1 / np.sqrt(S) * fs[:, None], "e4m3")
    return {
        "ta": (np.random.randint(-7, 8, (K, T)).astype(np.float64)).astype(np.float32),
        "ga": ((np.random.randint(8, 25, (K, 1)) / 64.0) * fk[:, None]).astype(np.float32),
        "w_words": wp[0],
        "w_scales": wp[1],
        "sa": (np.random.uniform(0.5, 1.6, (R, 1))).astype(np.float32),
        "sb": (np.random.uniform(0.5, 1.6, (R, 1))).astype(np.float32),
        "wb_words": wbp[0],
        "wb_scales": wbp[1],
        "xr_words": xrp[0],
        "xr_scales": xrp[1],
        "ws_words": wsp[0],
        "ws_scales": wsp[1],
        "so": (np.random.uniform(0.5, 1.6, (N, 1))).astype(np.float32),
        "sp": (np.random.uniform(0.5, 1.6, (N, 1))).astype(np.float32),
        "offs": striped8(idx),
        "offs2": striped8(idx2),
        "offs3": striped8(idx3),
        "offs4": striped8(idx4),
        "offs5": striped(idx5),
        "offs6": striped8(idx6),
        "offs7": striped(idx7),
    }


def reference(ta, ga, w_words, w_scales, sa, sb, wb_words, wb_scales, xr_words, xr_scales, ws_words, ws_scales, so, sp, offs, offs2, offs3, offs4, offs5, offs6, offs7):
    idx = unstriped8(offs)
    idx2 = unstriped8(offs2)
    idx3 = unstriped8(offs3)
    idx4 = unstriped8(offs4)
    idx5 = unstriped(offs5)
    idx6 = unstriped8(offs6)
    idx7 = unstriped(offs7)
    wu = unpack_weight(w_words, w_scales, "e4m3")
    wbu = unpack_weight(wb_words, wb_scales, "e2m1")
    xru = unpack_weight(xr_words, xr_scales, "e2m1")
    wsu = unpack_weight(ws_words, ws_scales, "e4m3")
    xc = pick8(f64(ta), idx, 64) * f64(ga)
    xcq = mxq(xc, 0, "e4m3")
    a = wu.T @ xcq
    pw = np.zeros((R, C))
    pw[np.arange(R)[:, None], idx2[np.arange(R) % 512 // 64]] = a
    hid = np.abs(pick8(pw, idx3, 64) * f64(sa) - pick8(pw, idx4, 64) * f64(sb))
    hidq = mxq(hid, 0, "e4m3")
    xridx5g = xru[:, idx5]
    p = wbu.T @ hidq + wsu.T @ xridx5g
    y = pick8(p, idx6, 16) * f64(so) - p[:, idx7] * f64(sp)
    return y

@@ -1,0 +1,235 @@
+from contextlib import ExitStack
+
+import concourse.mybir as mybir
+
+K, J, R, T, O, C, N, S, Z, U = 512, 512, 512, 2048, 256, 1024, 256, 512, 1024, 128
+FLOPS = 2 * K * R * J + 2 * R * N * O + 2 * S * N * O
+
+F32 = mybir.dt.float32
+BF16 = mybir.dt.bfloat16
+I32 = mybir.dt.int32
+U32 = mybir.dt.uint32
+U16 = mybir.dt.uint16
+U8 = mybir.dt.uint8
+FP8X4 = mybir.dt.float8_e4m3fn_x4
+FP4X4 = mybir.dt.float4_e2m1fn_x4
+COPY = mybir.ActivationFunctionType.Copy
+ABS = mybir.ActivationFunctionType.Abs
+SUB = mybir.AluOpType.subtract
+
+P = 128
+PACK = 4
+HEAD = 128
+HALF = O // 2
+
+
+def tile_picked_codes_plain_one_boardpair_reminder_onepair_kernel(
+    tc, ta, ga, w_words, w_scales, sa, sb, wb_words, wb_scales, xr_words, xr_scales,
+    ws_words, ws_scales, so, sp, offs, offs2, offs3, offs4, offs5, offs6, offs7, out,
+):
+    nc = tc.nc
+    with ExitStack() as ctx:
+        keep = ctx.enter_context(tc.tile_pool(name="keep", bufs=1))
+        reuse = ctx.enter_context(tc.tile_pool(name="reuse", bufs=1))
+        psum = ctx.enter_context(tc.psum_pool(name="psum", bufs=1))
+
+        def load_list(name, src):
+            held = keep.tile(list(src.shape), U16, name=name)
+            nc.sync.dma_start(held[:], src)
+            return held
+
+        def load_rows4(name, src):
+            held = keep.tile([P, PACK], F32, name=name)
+            nc.sync.dma_start(held[:], src.rearrange("(p t) o -> p (t o)", t=PACK))
+            return held
+
+        def load_rows2(name, src):
+            held = keep.tile([P, 2], F32, name=name)
+            with nc.allow_non_contiguous_dma(reason="one value a partition"):
+                nc.sync.dma_start(held[:], src.rearrange("(m p) o -> p (m o)", p=P))
+            return held
+
+        def cleared_plane(name, width):
+            held = keep.tile([P, width], U8, name=name, align_bytes=64)
+            nc.vector.memset(held[:].bitcast(I32), 0)
+            return held
+
+        def load_plane(held, src):
+            for q in range(4):
+                nc.sync.dma_start(held[32 * q : 32 * q + 4, :].bitcast(I32), src[0, 4 * q : 4 * q + 4, :].bitcast(I32))
+
+        w_plane_raw = cleared_plane("w_plane_raw", R)
+        xr_plane = cleared_plane("xr_plane", Z)
+        ws_plane = cleared_plane("ws_plane", N)
+        wb_plane = cleared_plane("wb_plane", N)
+
+        ta_rows = ta.rearrange("(p t) c -> p t c", t=PACK)
+        table = [keep.tile([P, T], F32, name="table%d" % t) for t in range(PACK)]
+        nc.sync.dma_start(table[0][:], ta_rows[:, 0, :])
+        list1 = load_list("list1", offs)
+        ga_t = load_rows4("ga_t", ga)
+        load_plane(w_plane_raw, w_scales)
+        for t in range(1, PACK):
+            nc.sync.dma_start(table[t][:], ta_rows[:, t, :])
+        w_raw = keep.tile([P, R], I32, name="w_raw")
+        nc.sync.dma_start(w_raw[:], w_words[0].rearrange("p n t -> p (n t)").bitcast(I32))
+        list2 = load_list("list2", offs2)
+        list3 = load_list("list3", offs3)
+        list4 = load_list("list4", offs4)
+        sa_t = load_rows4("sa_t", sa)
+        sb_t = load_rows4("sb_t", sb)
+        list5 = load_list("list5", offs5)
+        xr_table = keep.tile([P, Z], U16, name="xr_table")
+        nc.sync.dma_start(xr_table[:].bitcast(I32), xr_words[0].bitcast(I32))
+        load_plane(xr_plane, xr_scales)
+        ws_codes = keep.tile([P, N], I32, name="ws_codes", align_bytes=64)
+        nc.sync.dma_start(ws_codes[:], ws_words[0].rearrange("p n t -> p (n t)").bitcast(I32))
+        load_plane(ws_plane, ws_scales)
+        wb_codes = keep.tile([P, 2 * N], U8, name="wb_codes", align_bytes=64)
+        nc.sync.dma_start(wb_codes[:].bitcast(I32), wb_words[0].bitcast(I32))
+        load_plane(wb_plane, wb_scales)
+        list6 = load_list("list6", offs6)
+        list7 = load_list("list7", offs7)
+        so_t = load_rows2("so_t", so)
+        sp_t = load_rows2("sp_t", sp)
+
+        board = [keep.tile([P, C], F32, name="board%d" % t) for t in range(PACK)]
+        for t in range(PACK):
+            nc.vector.memset(board[t][:], 0.0)
+
+        w_plane = keep.tile([P, PACK, P], U8, name="w_plane", align_bytes=64)
+        nc.vector.tensor_copy(
+            out=w_plane[:].rearrange("p t m -> p m t"),
+            in_=w_plane_raw[:].rearrange("p (m t) -> p m t", t=PACK),
+        )
+
+        x_head = keep.tile([P, HEAD, PACK], BF16, name="x_head", align_bytes=64)
+        x_rest = keep.tile([P, J - HEAD, PACK], BF16, name="x_rest", align_bytes=64)
+        x_codes = keep.tile([P, J], U32, name="x_codes", align_bytes=64)
+        x_plane = keep.tile([P, J], U8, name="x_plane", align_bytes=64)
+        picked = [keep.tile([P, J], BF16, name="picked%d" % t) for t in range(PACK)]
+        for t in range(PACK):
+            nc.scalar.activation(out=picked[t][:], in_=table[t][:].indirect(list1[:]), func=COPY, scale=ga_t[:, t : t + 1])
+        for t in range(PACK - 1):
+            nc.vector.tensor_copy(out=x_head[:, :, t], in_=picked[t][:, :HEAD])
+            nc.vector.tensor_copy(out=x_rest[:, :, t], in_=picked[t][:, HEAD:])
+
+        w_codes = keep.tile([P, PACK, P], I32, name="w_codes", align_bytes=64)
+        nc.vector.tensor_copy(
+            out=w_codes[:].rearrange("p t m -> p m t"),
+            in_=w_raw[:].rearrange("p (m t) -> p m t", t=PACK),
+        )
+
+        last = PACK - 1
+        mid = (J - HEAD) // 2
+        nc.vector.tensor_copy(out=x_head[:, :, last], in_=picked[last][:, :HEAD])
+        nc.vector.tensor_copy(out=x_rest[:, :mid, last], in_=picked[last][:, HEAD : HEAD + mid])
+        nc.vector.quantize_mx(out=x_codes[:, :HEAD].bitcast(FP8X4), scales=x_plane[:, :HEAD],
+                              in_=x_head[:].rearrange("p j t -> p (j t)"))
+        nc.vector.tensor_copy(out=x_rest[:, mid:, last], in_=picked[last][:, HEAD + mid :])
+        nc.vector.quantize_mx(out=x_codes[:, HEAD:].bitcast(FP8X4), scales=x_plane[:, HEAD:],
+                              in_=x_rest[:].rearrange("p j t -> p (j t)"))
+
+        a_bank = [psum.tile([P, J], F32, name="a_bank%d" % t) for t in range(PACK)]
+
+        def first_product(t, lo, hi):
+            nc.tensor.matmul_mx(
+                out=a_bank[t][:, lo:hi],
+                lhsT=w_codes[:, t, :].bitcast(FP8X4), lhsT_scale=w_plane[:, t, :],
+                rhs=x_codes[:, lo:hi].bitcast(FP8X4), rhs_scale=x_plane[:, lo:hi],
+                start=True, stop=True,
+            )
+
+        pieces = [(0, 0, HEAD), (1, 0, HEAD), (0, HEAD, J), (1, HEAD, J), (2, 0, J), (3, 0, J)]
+        a_sb = {}
+        for t, lo, hi in pieces:
+            if t < 2:
+                a_sb[(t, lo)] = keep.tile([P, hi - lo], F32, name="a%d_%d" % (t, lo))
+        a_sb[(2, 0)] = reuse.tile([P, J], F32, name="a2", offset=0, align_bytes=64)
+        a_sb[(3, 0)] = reuse.tile([P, J], F32, name="a3", offset=4 * J, align_bytes=64)
+        for t, lo, hi in pieces:
+            if hi - lo == J - HEAD:
+                first_product(t, lo, 2 * HEAD)
+                first_product(t, 2 * HEAD, hi)
+            else:
+                first_product(t, lo, hi)
+            nc.scalar.copy(out=a_sb[(t, lo)][:], in_=a_bank[t][:, lo:hi])
+        for t, lo, hi in pieces:
+            nc.vector.tensor_copy(out=board[t][:].indirect(list2[:, lo // 16 : hi // 16]), in_=a_sb[(t, lo)][:])
+
+        read_a = keep.tile([P, PACK, O], F32, name="read_a")
+        read_b = keep.tile([P, PACK, O], F32, name="read_b")
+        hid = [keep.tile([P, HALF, PACK], BF16, name="hid%d" % h, align_bytes=64) for h in range(2)]
+
+        def read_board(t):
+            nc.scalar.activation(out=read_a[:, t, :], in_=board[t][:].indirect(list3[:]), func=COPY, scale=sa_t[:, t : t + 1])
+            nc.scalar.activation(out=read_b[:, t, :], in_=board[t][:].indirect(list4[:]), func=COPY, scale=sb_t[:, t : t + 1])
+
+        def magnitude(diff, pair, h):
+            nc.scalar.activation(
+                out=hid[h][:, :, 2 * pair : 2 * pair + 2],
+                in_=diff[:, :, h * HALF : (h + 1) * HALF].rearrange("p t o -> p o t"),
+                func=ABS,
+            )
+
+        read_board(0)
+        read_board(1)
+        read_board(2)
+        diff01 = reuse.tile([P, 2, O], F32, name="diff01", offset=0, align_bytes=64)
+        nc.vector.tensor_tensor(out=diff01[:], in0=read_a[:, 0:2, :], in1=read_b[:, 0:2, :], op=SUB)
+        for h in range(2):
+            magnitude(diff01, 0, h)
+        read_board(3)
+
+        xr_codes = reuse.tile([P, O], U16, name="xr_codes", offset=4 * J, align_bytes=64)
+        xr_picked_plane = reuse.tile([P, O], U8, name="xr_picked_plane", offset=4 * J + 2 * O, align_bytes=64)
+        nc.vector.tensor_copy(out=xr_codes[:], in_=xr_table[:].indirect(list5[:]))
+        nc.vector.tensor_copy(out=xr_picked_plane[:], in_=xr_plane[:].indirect(list5[:]))
+
+        p_bank = [[psum.tile([P, HALF], F32, name="p_bank%d%d" % (m, h)) for h in range(2)] for m in range(2)]
+        for h in range(2):
+            cols = slice(h * HALF, (h + 1) * HALF)
+            for m in range(2):
+                rows = slice(m * P, (m + 1) * P)
+                nc.tensor.matmul_mx(
+                    out=p_bank[m][h][:],
+                    lhsT=ws_codes[:, rows].bitcast(FP8X4), lhsT_scale=ws_plane[:, rows],
+                    rhs=xr_codes[:, cols].bitcast(FP4X4), rhs_scale=xr_picked_plane[:, cols],
+                    start=True, stop=False,
+                )
+
+        diff23 = keep.tile([P, 2, O], F32, name="diff23")
+        hid_codes = keep.tile([P, O], U32, name="hid_codes", align_bytes=64)
+        hid_plane = keep.tile([P, O], U8, name="hid_plane", align_bytes=64)
+        p_sb = [keep.tile([P, O], F32, name="p_sb%d" % m) for m in range(2)]
+        for h in range(2):
+            cols = slice(h * HALF, (h + 1) * HALF)
+            nc.vector.tensor_tensor(out=diff23[:, :, cols], in0=read_a[:, 2:4, cols], in1=read_b[:, 2:4, cols], op=SUB)
+        for h in range(2):
+            magnitude(diff23, 1, h)
+        for h in range(2):
+            cols = slice(h * HALF, (h + 1) * HALF)
+            nc.vector.quantize_mx(out=hid_codes[:, cols].bitcast(FP8X4), scales=hid_plane[:, cols],
+                                  in_=hid[h][:].rearrange("p o t -> p (o t)"))
+        for h in range(2):
+            cols = slice(h * HALF, (h + 1) * HALF)
+            for m in range(2):
+                nc.tensor.matmul_mx(
+                    out=p_bank[m][h][:],
+                    lhsT=wb_codes[:, 2 * m * P : 2 * (m + 1) * P].bitcast(FP4X4), lhsT_scale=wb_plane[:, m * P : (m + 1) * P],
+                    rhs=hid_codes[:, cols].bitcast(FP8X4), rhs_scale=hid_plane[:, cols],
+                    start=False, stop=True,
+                )
+        nc.vector.tensor_copy(out=p_sb[0][:, :HALF], in_=p_bank[0][0][:])
+        nc.vector.tensor_copy(out=p_sb[1][:, :HALF], in_=p_bank[1][0][:])
+        nc.scalar.copy(out=p_sb[0][:, HALF:], in_=p_bank[0][1][:])
+        nc.vector.tensor_copy(out=p_sb[1][:, HALF:], in_=p_bank[1][1][:])
+
+        for m in range(2):
+            first = keep.tile([P, U], F32, name="first%d" % m)
+            second = keep.tile([P, U], F32, name="second%d" % m)
+            result = keep.tile([P, U], F32, name="result%d" % m)
+            nc.scalar.activation(out=first[:], in_=p_sb[m][:].indirect(list6[:]), func=COPY, scale=so_t[:, m : m + 1])
+            nc.scalar.activation(out=second[:], in_=p_sb[m][:].indirect(list7[:]), func=COPY, scale=sp_t[:, m : m + 1])
+            nc.vector.tensor_tensor(out=result[:], in0=first[:], in1=second[:], op=SUB)
+            nc.sync.dma_start(out[m * P : (m + 1) * P, :], result[:])

@@ -16,11 +16,14 @@ FP4X4 = mybir.dt.float4_e2m1fn_x4
 COPY = mybir.ActivationFunctionType.Copy
 ABS = mybir.ActivationFunctionType.Abs
 SUB = mybir.AluOpType.subtract
+MULT = mybir.AluOpType.mult
+MAX = mybir.AluOpType.max
 
 P = 128
 PACK = 4
 HEAD = 128
 HALF = O // 2
+RING = 3
 
 
 def tile_picked_codes_plain_one_boardpair_reminder_onepair_kernel(
@@ -131,39 +134,38 @@ def tile_picked_codes_plain_one_boardpair_reminder_onepair_kernel(
                               in_=x_rest[:].rearrange("p j t -> p (j t)"))
 
         a_bank = [psum.tile([P, J], F32, name="a_bank%d" % t) for t in range(PACK)]
+        head_bank = [psum.tile([P, HEAD], F32, name="head_bank%d" % t, tag="small%d" % t) for t in range(2)]
 
-        def first_product(t, lo, hi):
+        def first_product(bank, t, lo, hi):
             nc.tensor.matmul_mx(
-                out=a_bank[t][:, lo:hi],
+                out=bank[:, lo:hi],
                 lhsT=w_codes[:, t, :].bitcast(FP8X4), lhsT_scale=w_plane[:, t, :],
                 rhs=x_codes[:, lo:hi].bitcast(FP8X4), rhs_scale=x_plane[:, lo:hi],
                 start=True, stop=True,
             )
 
         pieces = [(0, 0, HEAD), (1, 0, HEAD), (0, HEAD, J), (1, HEAD, J), (2, 0, J), (3, 0, J)]
-        a_sb = {}
         for t, lo, hi in pieces:
-            if t < 2:
-                a_sb[(t, lo)] = keep.tile([P, hi - lo], F32, name="a%d_%d" % (t, lo))
-        a_sb[(2, 0)] = reuse.tile([P, J], F32, name="a2", offset=0, align_bytes=64)
-        a_sb[(3, 0)] = reuse.tile([P, J], F32, name="a3", offset=4 * J, align_bytes=64)
-        for t, lo, hi in pieces:
+            bank = head_bank[t] if hi == HEAD else a_bank[t]
             if hi - lo == J - HEAD:
-                first_product(t, lo, 2 * HEAD)
-                first_product(t, 2 * HEAD, hi)
+                first_product(bank, t, lo, 2 * HEAD)
+                first_product(bank, t, 2 * HEAD, hi)
             else:
-                first_product(t, lo, hi)
-            nc.scalar.copy(out=a_sb[(t, lo)][:], in_=a_bank[t][:, lo:hi])
-        for t, lo, hi in pieces:
-            nc.vector.tensor_copy(out=board[t][:].indirect(list2[:, lo // 16 : hi // 16]), in_=a_sb[(t, lo)][:])
+                first_product(bank, t, lo, hi)
+        for n, (t, lo, hi) in enumerate(pieces):
+            bank = head_bank[t] if hi == HEAD else a_bank[t]
+            piece = reuse.tile([P, hi - lo], F32, name="piece%d" % n, offset=(n % RING) * 4 * J, align_bytes=64)
+            nc.scalar.copy(out=piece[:], in_=bank[:, lo:hi])
+            nc.vector.tensor_copy(out=board[t][:].indirect(list2[:, lo // 16 : hi // 16]), in_=piece[:])
+        last_slot = ((len(pieces) - 1) % RING) * 4 * J
 
-        read_a = keep.tile([P, PACK, O], F32, name="read_a")
-        read_b = keep.tile([P, PACK, O], F32, name="read_b")
+        read_a = [keep.tile([P, O], F32, name="read_a%d" % t) for t in range(PACK - 1)]
+        read_b = [keep.tile([P, O], F32, name="read_b%d" % t) for t in range(PACK - 1)]
         hid = [keep.tile([P, HALF, PACK], BF16, name="hid%d" % h, align_bytes=64) for h in range(2)]
 
         def read_board(t):
-            nc.scalar.activation(out=read_a[:, t, :], in_=board[t][:].indirect(list3[:]), func=COPY, scale=sa_t[:, t : t + 1])
-            nc.scalar.activation(out=read_b[:, t, :], in_=board[t][:].indirect(list4[:]), func=COPY, scale=sb_t[:, t : t + 1])
+            nc.scalar.activation(out=read_a[t][:], in_=board[t][:].indirect(list3[:]), func=COPY, scale=sa_t[:, t : t + 1])
+            nc.scalar.activation(out=read_b[t][:], in_=board[t][:].indirect(list4[:]), func=COPY, scale=sb_t[:, t : t + 1])
 
         def magnitude(diff, pair, h):
             nc.scalar.activation(
@@ -172,21 +174,24 @@ def tile_picked_codes_plain_one_boardpair_reminder_onepair_kernel(
                 func=ABS,
             )
 
-        read_board(0)
-        read_board(1)
-        read_board(2)
-        diff01 = reuse.tile([P, 2, O], F32, name="diff01", offset=0, align_bytes=64)
-        nc.vector.tensor_tensor(out=diff01[:], in0=read_a[:, 0:2, :], in1=read_b[:, 0:2, :], op=SUB)
+        diff01 = reuse.tile([P, 2, O], F32, name="diff01", offset=RING * 4 * J, align_bytes=64)
+        diff23 = keep.tile([P, 2, O], F32, name="diff23")
+        for t in range(PACK - 1):
+            read_board(t)
+            diff = diff01 if t < 2 else diff23
+            nc.gpsimd.tensor_tensor(out=diff[:, t % 2, :], in0=read_a[t][:], in1=read_b[t][:], op=SUB)
         for h in range(2):
             magnitude(diff01, 0, h)
+        read_a.append(reuse.tile([P, O], F32, name="read_a3", offset=RING * 4 * J, align_bytes=64))
+        read_b.append(reuse.tile([P, O], F32, name="read_b3", offset=RING * 4 * J + 4 * O, align_bytes=64))
         read_board(3)
 
-        xr_codes = reuse.tile([P, O], U16, name="xr_codes", offset=4 * J, align_bytes=64)
-        xr_picked_plane = reuse.tile([P, O], U8, name="xr_picked_plane", offset=4 * J + 2 * O, align_bytes=64)
+        xr_codes = reuse.tile([P, O], U16, name="xr_codes", offset=last_slot, align_bytes=64)
+        xr_picked_plane = reuse.tile([P, O], U8, name="xr_picked_plane", offset=last_slot + 2 * O, align_bytes=64)
         nc.vector.tensor_copy(out=xr_codes[:], in_=xr_table[:].indirect(list5[:]))
         nc.vector.tensor_copy(out=xr_picked_plane[:], in_=xr_plane[:].indirect(list5[:]))
 
-        p_bank = [[psum.tile([P, HALF], F32, name="p_bank%d%d" % (m, h)) for h in range(2)] for m in range(2)]
+        p_bank = [[psum.tile([P, HALF], F32, name="p_bank%d%d" % (m, h), tag="small%d" % (2 * h + m)) for h in range(2)] for m in range(2)]
         for h in range(2):
             cols = slice(h * HALF, (h + 1) * HALF)
             for m in range(2):
@@ -198,22 +203,22 @@ def tile_picked_codes_plain_one_boardpair_reminder_onepair_kernel(
                     start=True, stop=False,
                 )
 
-        diff23 = keep.tile([P, 2, O], F32, name="diff23")
         hid_codes = keep.tile([P, O], U32, name="hid_codes", align_bytes=64)
         hid_plane = keep.tile([P, O], U8, name="hid_plane", align_bytes=64)
         p_sb = [keep.tile([P, O], F32, name="p_sb%d" % m) for m in range(2)]
         for h in range(2):
             cols = slice(h * HALF, (h + 1) * HALF)
-            nc.vector.tensor_tensor(out=diff23[:, :, cols], in0=read_a[:, 2:4, cols], in1=read_b[:, 2:4, cols], op=SUB)
-        for h in range(2):
-            magnitude(diff23, 1, h)
+            nc.vector.tensor_tensor(out=diff23[:, 1, cols], in0=read_a[3][:, cols], in1=read_b[3][:, cols], op=SUB)
+        magnitude(diff23, 1, 0)
+        late = diff23[:, :, HALF:].rearrange("p t o -> p o t")
+        nc.vector.scalar_tensor_tensor(out=hid[1][:, :, 2:4], in0=late, scalar=-1.0, in1=late, op0=MULT, op1=MAX)
         for h in range(2):
             cols = slice(h * HALF, (h + 1) * HALF)
             nc.vector.quantize_mx(out=hid_codes[:, cols].bitcast(FP8X4), scales=hid_plane[:, cols],
                                   in_=hid[h][:].rearrange("p o t -> p (o t)"))
-        for h in range(2):
-            cols = slice(h * HALF, (h + 1) * HALF)
-            for m in range(2):
+        for m in range(2):
+            for h in range(2):
+                cols = slice(h * HALF, (h + 1) * HALF)
                 nc.tensor.matmul_mx(
                     out=p_bank[m][h][:],
                     lhsT=wb_codes[:, 2 * m * P : 2 * (m + 1) * P].bitcast(FP4X4), lhsT_scale=wb_plane[:, m * P : (m + 1) * P],
@@ -221,8 +226,8 @@ def tile_picked_codes_plain_one_boardpair_reminder_onepair_kernel(
                     start=False, stop=True,
                 )
         nc.vector.tensor_copy(out=p_sb[0][:, :HALF], in_=p_bank[0][0][:])
-        nc.vector.tensor_copy(out=p_sb[1][:, :HALF], in_=p_bank[1][0][:])
         nc.scalar.copy(out=p_sb[0][:, HALF:], in_=p_bank[0][1][:])
+        nc.vector.tensor_copy(out=p_sb[1][:, :HALF], in_=p_bank[1][0][:])
         nc.vector.tensor_copy(out=p_sb[1][:, HALF:], in_=p_bank[1][1][:])
 
         for m in range(2):

@@ -21,9 +21,13 @@ MAX = mybir.AluOpType.max
 
 P = 128
 PACK = 4
+QUADRANT = 32
+PER_COLUMN = 16
 HEAD = 128
 HALF = O // 2
 RING = 3
+SLOT = 4 * J
+ROW = 4 * O
 
 
 def tile_picked_codes_plain_one_boardpair_reminder_onepair_kernel(
@@ -58,8 +62,11 @@ def tile_picked_codes_plain_one_boardpair_reminder_onepair_kernel(
             return held
 
         def load_plane(held, src):
-            for q in range(4):
-                nc.sync.dma_start(held[32 * q : 32 * q + 4, :].bitcast(I32), src[0, 4 * q : 4 * q + 4, :].bitcast(I32))
+            for q in range(P // QUADRANT):
+                nc.sync.dma_start(
+                    held[QUADRANT * q : QUADRANT * q + PACK, :].bitcast(I32),
+                    src[0, PACK * q : PACK * (q + 1), :].bitcast(I32),
+                )
 
         w_plane_raw = cleared_plane("w_plane_raw", R)
         xr_plane = cleared_plane("xr_plane", Z)
@@ -154,10 +161,10 @@ def tile_picked_codes_plain_one_boardpair_reminder_onepair_kernel(
                 first_product(bank, t, lo, hi)
         for n, (t, lo, hi) in enumerate(pieces):
             bank = head_bank[t] if hi == HEAD else a_bank[t]
-            piece = reuse.tile([P, hi - lo], F32, name="piece%d" % n, offset=(n % RING) * 4 * J, align_bytes=64)
+            piece = reuse.tile([P, hi - lo], F32, name="piece%d" % n, offset=(n % RING) * SLOT, align_bytes=64)
             nc.scalar.copy(out=piece[:], in_=bank[:, lo:hi])
-            nc.vector.tensor_copy(out=board[t][:].indirect(list2[:, lo // 16 : hi // 16]), in_=piece[:])
-        last_slot = ((len(pieces) - 1) % RING) * 4 * J
+            nc.vector.tensor_copy(out=board[t][:].indirect(list2[:, lo // PER_COLUMN : hi // PER_COLUMN]), in_=piece[:])
+        last_slot = ((len(pieces) - 1) % RING) * SLOT
 
         read_a = [keep.tile([P, O], F32, name="read_a%d" % t) for t in range(PACK - 1)]
         read_b = [keep.tile([P, O], F32, name="read_b%d" % t) for t in range(PACK - 1)]
@@ -174,7 +181,7 @@ def tile_picked_codes_plain_one_boardpair_reminder_onepair_kernel(
                 func=ABS,
             )
 
-        diff01 = reuse.tile([P, 2, O], F32, name="diff01", offset=RING * 4 * J, align_bytes=64)
+        diff01 = reuse.tile([P, 2, O], F32, name="diff01", offset=RING * SLOT, align_bytes=64)
         diff23 = keep.tile([P, 2, O], F32, name="diff23")
         for t in range(PACK - 1):
             read_board(t)
@@ -182,16 +189,19 @@ def tile_picked_codes_plain_one_boardpair_reminder_onepair_kernel(
             nc.gpsimd.tensor_tensor(out=diff[:, t % 2, :], in0=read_a[t][:], in1=read_b[t][:], op=SUB)
         for h in range(2):
             magnitude(diff01, 0, h)
-        read_a.append(reuse.tile([P, O], F32, name="read_a3", offset=RING * 4 * J, align_bytes=64))
-        read_b.append(reuse.tile([P, O], F32, name="read_b3", offset=RING * 4 * J + 4 * O, align_bytes=64))
-        read_board(3)
+        read_a.append(reuse.tile([P, O], F32, name="read_a3", offset=RING * SLOT, align_bytes=64))
+        read_b.append(reuse.tile([P, O], F32, name="read_b3", offset=RING * SLOT + ROW, align_bytes=64))
+        read_board(last)
 
         xr_codes = reuse.tile([P, O], U16, name="xr_codes", offset=last_slot, align_bytes=64)
         xr_picked_plane = reuse.tile([P, O], U8, name="xr_picked_plane", offset=last_slot + 2 * O, align_bytes=64)
         nc.vector.tensor_copy(out=xr_codes[:], in_=xr_table[:].indirect(list5[:]))
         nc.vector.tensor_copy(out=xr_picked_plane[:], in_=xr_plane[:].indirect(list5[:]))
 
-        p_bank = [[psum.tile([P, HALF], F32, name="p_bank%d%d" % (m, h), tag="small%d" % (2 * h + m)) for h in range(2)] for m in range(2)]
+        p_bank = [
+            [psum.tile([P, HALF], F32, name="p_bank%d%d" % (m, h), tag="small%d" % (2 * h + m)) for h in range(2)]
+            for m in range(2)
+        ]
         for h in range(2):
             cols = slice(h * HALF, (h + 1) * HALF)
             for m in range(2):
@@ -208,7 +218,7 @@ def tile_picked_codes_plain_one_boardpair_reminder_onepair_kernel(
         p_sb = [keep.tile([P, O], F32, name="p_sb%d" % m) for m in range(2)]
         for h in range(2):
             cols = slice(h * HALF, (h + 1) * HALF)
-            nc.vector.tensor_tensor(out=diff23[:, 1, cols], in0=read_a[3][:, cols], in1=read_b[3][:, cols], op=SUB)
+            nc.vector.tensor_tensor(out=diff23[:, 1, cols], in0=read_a[last][:, cols], in1=read_b[last][:, cols], op=SUB)
         magnitude(diff23, 1, 0)
         late = diff23[:, :, HALF:].rearrange("p t o -> p o t")
         nc.vector.scalar_tensor_tensor(out=hid[1][:, :, 2:4], in0=late, scalar=-1.0, in1=late, op0=MULT, op1=MAX)
@@ -221,7 +231,8 @@ def tile_picked_codes_plain_one_boardpair_reminder_onepair_kernel(
                 cols = slice(h * HALF, (h + 1) * HALF)
                 nc.tensor.matmul_mx(
                     out=p_bank[m][h][:],
-                    lhsT=wb_codes[:, 2 * m * P : 2 * (m + 1) * P].bitcast(FP4X4), lhsT_scale=wb_plane[:, m * P : (m + 1) * P],
+                    lhsT=wb_codes[:, 2 * m * P : 2 * (m + 1) * P].bitcast(FP4X4),
+                    lhsT_scale=wb_plane[:, m * P : (m + 1) * P],
                     rhs=hid_codes[:, cols].bitcast(FP8X4), rhs_scale=hid_plane[:, cols],
                     start=False, stop=True,
                 )

from contextlib import ExitStack

import concourse.mybir as mybir

K, J, R, T, O, C, N, S, Z, U = 512, 512, 512, 2048, 256, 1024, 256, 512, 1024, 128
FLOPS = 2 * K * R * J + 2 * R * N * O + 2 * S * N * O

F32 = mybir.dt.float32
BF16 = mybir.dt.bfloat16
I32 = mybir.dt.int32
U32 = mybir.dt.uint32
U16 = mybir.dt.uint16
U8 = mybir.dt.uint8
FP8X4 = mybir.dt.float8_e4m3fn_x4
FP4X4 = mybir.dt.float4_e2m1fn_x4
COPY = mybir.ActivationFunctionType.Copy
ABS = mybir.ActivationFunctionType.Abs
SUB = mybir.AluOpType.subtract
MULT = mybir.AluOpType.mult
MAX = mybir.AluOpType.max

P = 128
PACK = 4
QUADRANT = 32
PER_COLUMN = 16
HEAD = 128
HALF = O // 2
RING = 3
SLOT = 4 * J
ROW = 4 * O


def tile_picked_codes_plain_one_boardpair_reminder_onepair_kernel(
    tc, ta, ga, w_words, w_scales, sa, sb, wb_words, wb_scales, xr_words, xr_scales,
    ws_words, ws_scales, so, sp, offs, offs2, offs3, offs4, offs5, offs6, offs7, out,
):
    nc = tc.nc
    with ExitStack() as ctx:
        keep = ctx.enter_context(tc.tile_pool(name="keep", bufs=1))
        reuse = ctx.enter_context(tc.tile_pool(name="reuse", bufs=1))
        psum = ctx.enter_context(tc.psum_pool(name="psum", bufs=1))

        def load_list(name, src):
            held = keep.tile(list(src.shape), U16, name=name)
            nc.sync.dma_start(held[:], src)
            return held

        def load_rows4(name, src):
            held = keep.tile([P, PACK], F32, name=name)
            nc.sync.dma_start(held[:], src.rearrange("(p t) o -> p (t o)", t=PACK))
            return held

        def load_rows2(name, src):
            held = keep.tile([P, 2], F32, name=name)
            with nc.allow_non_contiguous_dma(reason="one value a partition"):
                nc.sync.dma_start(held[:], src.rearrange("(m p) o -> p (m o)", p=P))
            return held

        def cleared_plane(name, width):
            held = keep.tile([P, width], U8, name=name, align_bytes=64)
            nc.vector.memset(held[:].bitcast(I32), 0)
            return held

        def load_plane(held, src):
            for q in range(P // QUADRANT):
                nc.sync.dma_start(
                    held[QUADRANT * q : QUADRANT * q + PACK, :].bitcast(I32),
                    src[0, PACK * q : PACK * (q + 1), :].bitcast(I32),
                )

        w_plane_raw = cleared_plane("w_plane_raw", R)
        xr_plane = cleared_plane("xr_plane", Z)
        ws_plane = cleared_plane("ws_plane", N)
        wb_plane = cleared_plane("wb_plane", N)

        ta_rows = ta.rearrange("(p t) c -> p t c", t=PACK)
        table = [keep.tile([P, T], F32, name="table%d" % t) for t in range(PACK)]
        nc.sync.dma_start(table[0][:], ta_rows[:, 0, :])
        list1 = load_list("list1", offs)
        ga_t = load_rows4("ga_t", ga)
        load_plane(w_plane_raw, w_scales)
        for t in range(1, PACK):
            nc.sync.dma_start(table[t][:], ta_rows[:, t, :])
        w_raw = keep.tile([P, R], I32, name="w_raw")
        nc.sync.dma_start(w_raw[:], w_words[0].rearrange("p n t -> p (n t)").bitcast(I32))
        list2 = load_list("list2", offs2)
        list3 = load_list("list3", offs3)
        list4 = load_list("list4", offs4)
        sa_t = load_rows4("sa_t", sa)
        sb_t = load_rows4("sb_t", sb)
        list5 = load_list("list5", offs5)
        xr_table = keep.tile([P, Z], U16, name="xr_table")
        nc.sync.dma_start(xr_table[:].bitcast(I32), xr_words[0].bitcast(I32))
        load_plane(xr_plane, xr_scales)
        ws_codes = keep.tile([P, N], I32, name="ws_codes", align_bytes=64)
        nc.sync.dma_start(ws_codes[:], ws_words[0].rearrange("p n t -> p (n t)").bitcast(I32))
        load_plane(ws_plane, ws_scales)
        wb_codes = keep.tile([P, 2 * N], U8, name="wb_codes", align_bytes=64)
        nc.sync.dma_start(wb_codes[:].bitcast(I32), wb_words[0].bitcast(I32))
        load_plane(wb_plane, wb_scales)
        list6 = load_list("list6", offs6)
        list7 = load_list("list7", offs7)
        so_t = load_rows2("so_t", so)
        sp_t = load_rows2("sp_t", sp)

        board = [keep.tile([P, C], F32, name="board%d" % t) for t in range(PACK)]
        for t in range(PACK):
            nc.vector.memset(board[t][:], 0.0)

        w_plane = keep.tile([P, PACK, P], U8, name="w_plane", align_bytes=64)
        nc.vector.tensor_copy(
            out=w_plane[:].rearrange("p t m -> p m t"),
            in_=w_plane_raw[:].rearrange("p (m t) -> p m t", t=PACK),
        )

        x_head = keep.tile([P, HEAD, PACK], BF16, name="x_head", align_bytes=64)
        x_rest = keep.tile([P, J - HEAD, PACK], BF16, name="x_rest", align_bytes=64)
        x_codes = keep.tile([P, J], U32, name="x_codes", align_bytes=64)
        x_plane = keep.tile([P, J], U8, name="x_plane", align_bytes=64)
        picked = [keep.tile([P, J], BF16, name="picked%d" % t) for t in range(PACK)]
        for t in range(PACK):
            nc.scalar.activation(out=picked[t][:], in_=table[t][:].indirect(list1[:]), func=COPY, scale=ga_t[:, t : t + 1])
        for t in range(PACK - 1):
            nc.vector.tensor_copy(out=x_head[:, :, t], in_=picked[t][:, :HEAD])
            nc.vector.tensor_copy(out=x_rest[:, :, t], in_=picked[t][:, HEAD:])

        w_codes = keep.tile([P, PACK, P], I32, name="w_codes", align_bytes=64)
        nc.vector.tensor_copy(
            out=w_codes[:].rearrange("p t m -> p m t"),
            in_=w_raw[:].rearrange("p (m t) -> p m t", t=PACK),
        )

        last = PACK - 1
        mid = (J - HEAD) // 2
        nc.vector.tensor_copy(out=x_head[:, :, last], in_=picked[last][:, :HEAD])
        nc.vector.tensor_copy(out=x_rest[:, :mid, last], in_=picked[last][:, HEAD : HEAD + mid])
        nc.vector.quantize_mx(out=x_codes[:, :HEAD].bitcast(FP8X4), scales=x_plane[:, :HEAD],
                              in_=x_head[:].rearrange("p j t -> p (j t)"))
        nc.vector.tensor_copy(out=x_rest[:, mid:, last], in_=picked[last][:, HEAD + mid :])
        nc.vector.quantize_mx(out=x_codes[:, HEAD:].bitcast(FP8X4), scales=x_plane[:, HEAD:],
                              in_=x_rest[:].rearrange("p j t -> p (j t)"))

        a_bank = [psum.tile([P, J], F32, name="a_bank%d" % t) for t in range(PACK)]
        head_bank = [psum.tile([P, HEAD], F32, name="head_bank%d" % t, tag="small%d" % t) for t in range(2)]

        def first_product(bank, t, lo, hi):
            nc.tensor.matmul_mx(
                out=bank[:, lo:hi],
                lhsT=w_codes[:, t, :].bitcast(FP8X4), lhsT_scale=w_plane[:, t, :],
                rhs=x_codes[:, lo:hi].bitcast(FP8X4), rhs_scale=x_plane[:, lo:hi],
                start=True, stop=True,
            )

        pieces = [(0, 0, HEAD), (1, 0, HEAD), (0, HEAD, J), (1, HEAD, J), (2, 0, J), (3, 0, J)]
        for t, lo, hi in pieces:
            bank = head_bank[t] if hi == HEAD else a_bank[t]
            if hi - lo == J - HEAD:
                first_product(bank, t, lo, 2 * HEAD)
                first_product(bank, t, 2 * HEAD, hi)
            else:
                first_product(bank, t, lo, hi)
        for n, (t, lo, hi) in enumerate(pieces):
            bank = head_bank[t] if hi == HEAD else a_bank[t]
            piece = reuse.tile([P, hi - lo], F32, name="piece%d" % n, offset=(n % RING) * SLOT, align_bytes=64)
            nc.scalar.copy(out=piece[:], in_=bank[:, lo:hi])
            nc.vector.tensor_copy(out=board[t][:].indirect(list2[:, lo // PER_COLUMN : hi // PER_COLUMN]), in_=piece[:])
        last_slot = ((len(pieces) - 1) % RING) * SLOT

        read_a = [keep.tile([P, O], F32, name="read_a%d" % t) for t in range(PACK - 1)]
        read_b = [keep.tile([P, O], F32, name="read_b%d" % t) for t in range(PACK - 1)]
        hid = [keep.tile([P, HALF, PACK], BF16, name="hid%d" % h, align_bytes=64) for h in range(2)]

        def read_board(t):
            nc.scalar.activation(out=read_a[t][:], in_=board[t][:].indirect(list3[:]), func=COPY, scale=sa_t[:, t : t + 1])
            nc.scalar.activation(out=read_b[t][:], in_=board[t][:].indirect(list4[:]), func=COPY, scale=sb_t[:, t : t + 1])

        def magnitude(diff, pair, h):
            nc.scalar.activation(
                out=hid[h][:, :, 2 * pair : 2 * pair + 2],
                in_=diff[:, :, h * HALF : (h + 1) * HALF].rearrange("p t o -> p o t"),
                func=ABS,
            )

        diff01 = reuse.tile([P, 2, O], F32, name="diff01", offset=RING * SLOT, align_bytes=64)
        diff23 = keep.tile([P, 2, O], F32, name="diff23")
        for t in range(PACK - 1):
            read_board(t)
            diff = diff01 if t < 2 else diff23
            nc.gpsimd.tensor_tensor(out=diff[:, t % 2, :], in0=read_a[t][:], in1=read_b[t][:], op=SUB)
        for h in range(2):
            magnitude(diff01, 0, h)
        read_a.append(reuse.tile([P, O], F32, name="read_a3", offset=RING * SLOT, align_bytes=64))
        read_b.append(reuse.tile([P, O], F32, name="read_b3", offset=RING * SLOT + ROW, align_bytes=64))
        read_board(last)

        xr_codes = reuse.tile([P, O], U16, name="xr_codes", offset=last_slot, align_bytes=64)
        xr_picked_plane = reuse.tile([P, O], U8, name="xr_picked_plane", offset=last_slot + 2 * O, align_bytes=64)
        nc.vector.tensor_copy(out=xr_codes[:], in_=xr_table[:].indirect(list5[:]))
        nc.vector.tensor_copy(out=xr_picked_plane[:], in_=xr_plane[:].indirect(list5[:]))

        p_bank = [
            [psum.tile([P, HALF], F32, name="p_bank%d%d" % (m, h), tag="small%d" % (2 * h + m)) for h in range(2)]
            for m in range(2)
        ]
        for h in range(2):
            cols = slice(h * HALF, (h + 1) * HALF)
            for m in range(2):
                rows = slice(m * P, (m + 1) * P)
                nc.tensor.matmul_mx(
                    out=p_bank[m][h][:],
                    lhsT=ws_codes[:, rows].bitcast(FP8X4), lhsT_scale=ws_plane[:, rows],
                    rhs=xr_codes[:, cols].bitcast(FP4X4), rhs_scale=xr_picked_plane[:, cols],
                    start=True, stop=False,
                )

        hid_codes = keep.tile([P, O], U32, name="hid_codes", align_bytes=64)
        hid_plane = keep.tile([P, O], U8, name="hid_plane", align_bytes=64)
        p_sb = [keep.tile([P, O], F32, name="p_sb%d" % m) for m in range(2)]
        for h in range(2):
            cols = slice(h * HALF, (h + 1) * HALF)
            nc.vector.tensor_tensor(out=diff23[:, 1, cols], in0=read_a[last][:, cols], in1=read_b[last][:, cols], op=SUB)
        magnitude(diff23, 1, 0)
        late = diff23[:, :, HALF:].rearrange("p t o -> p o t")
        nc.vector.scalar_tensor_tensor(out=hid[1][:, :, 2:4], in0=late, scalar=-1.0, in1=late, op0=MULT, op1=MAX)
        for h in range(2):
            cols = slice(h * HALF, (h + 1) * HALF)
            nc.vector.quantize_mx(out=hid_codes[:, cols].bitcast(FP8X4), scales=hid_plane[:, cols],
                                  in_=hid[h][:].rearrange("p o t -> p (o t)"))
        for m in range(2):
            for h in range(2):
                cols = slice(h * HALF, (h + 1) * HALF)
                nc.tensor.matmul_mx(
                    out=p_bank[m][h][:],
                    lhsT=wb_codes[:, 2 * m * P : 2 * (m + 1) * P].bitcast(FP4X4),
                    lhsT_scale=wb_plane[:, m * P : (m + 1) * P],
                    rhs=hid_codes[:, cols].bitcast(FP8X4), rhs_scale=hid_plane[:, cols],
                    start=False, stop=True,
                )
        nc.vector.tensor_copy(out=p_sb[0][:, :HALF], in_=p_bank[0][0][:])
        nc.scalar.copy(out=p_sb[0][:, HALF:], in_=p_bank[0][1][:])
        nc.vector.tensor_copy(out=p_sb[1][:, :HALF], in_=p_bank[1][0][:])
        nc.vector.tensor_copy(out=p_sb[1][:, HALF:], in_=p_bank[1][1][:])

        for m in range(2):
            first = keep.tile([P, U], F32, name="first%d" % m)
            second = keep.tile([P, U], F32, name="second%d" % m)
            result = keep.tile([P, U], F32, name="result%d" % m)
            nc.scalar.activation(out=first[:], in_=p_sb[m][:].indirect(list6[:]), func=COPY, scale=so_t[:, m : m + 1])
            nc.scalar.activation(out=second[:], in_=p_sb[m][:].indirect(list7[:]), func=COPY, scale=sp_t[:, m : m + 1])
            nc.vector.tensor_tensor(out=result[:], in0=first[:], in1=second[:], op=SUB)
            nc.sync.dma_start(out[m * P : (m + 1) * P, :], result[:])
